import numpy as np
import ml_dtypes


def mxq(x, axis, fmt="e4m3"):
    dtype, down = {"e4m3": (ml_dtypes.float8_e4m3fn, 7), "e5m2": (ml_dtypes.float8_e5m2, 14)}[fmt]
    v = np.moveaxis(np.asarray(x, np.float32).astype(ml_dtypes.bfloat16).astype(np.float64), axis, -1)
    blocks = v.reshape(v.shape[:-1] + (-1, 32))
    amax = np.abs(blocks).max(-1, keepdims=True)
    byte = np.maximum(np.where(amax > 0, np.frexp(amax)[1] - 1 + 127, 0) - down, 1)
    scale = np.exp2(byte - 127.0)
    codes = (blocks / scale).astype(np.float32).astype(dtype).astype(np.float64)
    return np.moveaxis((codes * scale).reshape(v.shape), -1, axis)


WIDE = False


def mx_kscale(k):
    if not WIDE:
        return np.ones(k)
    levels = np.array([10, -10, 5, -5, 0])
    if k % 512:
        return np.exp2(np.random.permutation(np.resize(levels, k // 32))).repeat(32)
    a = np.empty((k // 512, 16))
    for p in range(k // 512):
        a[p, :8] = np.random.permutation(np.resize(levels, 8))
        for g in range(8):
            far = levels[np.abs(levels - a[p, g]) >= 10]
            a[p, g + 8] = far[np.random.randint(len(far))]
    return np.exp2(a.ravel()).repeat(32)


def f64(x):
    return np.asarray(x).astype(np.float64)


def striped(idx):
    return np.tile(idx.reshape(-1, 16).T, (8, 1)).astype(np.uint16)


def unstriped(offs):
    return offs[:16].T.reshape(-1).astype(np.int64)


E2M1 = np.array([0.0, 0.5, 1.0, 1.5, 2.0, 3.0, 4.0, 6.0, -0.0, -0.5, -1.0, -1.5, -2.0, -3.0, -4.0, -6.0])


def pack_weight(w, fmt):
    k, n = w.shape
    w = f64(np.asarray(w, np.float32).astype(ml_dtypes.bfloat16)).reshape(k // 32, 32, n)
    amax = np.abs(w).max(1)
    if fmt == "e4m3":
        byte = np.frexp(amax)[1] - 1 + 127 - 7
    else:
        mant, ex = np.frexp(amax / 6.0)
        byte = np.where(mant > 0.5, ex, ex - 1) + 127
    byte = np.clip(np.where(amax > 0, byte, 1), 1, 254)
    scaled = (w * np.exp2(127.0 - byte)[:, None, :]).reshape(k, n).astype(np.float32)
    by_word = np.ascontiguousarray(scaled.reshape(k // 512, 128, 4, n).transpose(0, 1, 3, 2))
    if fmt == "e4m3":
        words = by_word.astype(ml_dtypes.float8_e4m3fn).view(np.uint8)
    else:
        c = by_word.astype(ml_dtypes.float4_e2m1fn).view(np.uint8) & 0xF
        words = (c[..., 0::2] | (c[..., 1::2] << 4)).reshape(k // 512, 128, 2 * n)
    return np.ascontiguousarray(words), np.ascontiguousarray(byte.astype(np.uint8).reshape(k // 512, 16, n))


def unpack_weight(words, scales, fmt):
    g, _, n = scales.shape
    words = np.ascontiguousarray(words).reshape(g, 128, n, -1)
    if fmt == "e4m3":
        vals = words.view(ml_dtypes.float8_e4m3fn).astype(np.float64)
    else:
        nib = np.empty((g, 128, n, 4), np.uint8)
        nib[..., 0::2] = words & 0xF
        nib[..., 1::2] = words >> 4
        vals = E2M1[nib]
    vals = vals * np.repeat(np.exp2(scales.astype(np.float64) - 127.0), 8, axis=1)[..., None]
    return vals.transpose(0, 1, 3, 2).reshape(g * 512, n)


def gelu(v):
    return 0.5 * v * (1.0 + np.tanh(np.sqrt(2.0 / np.pi) * (v + 0.044715 * v**3)))


K, T, S, S2 = 1024, 2048, 512, 1024

def setup_inputs():
    n = np.random.standard_normal
    s = mx_kscale(K)[:, None]
    d = {}
    d["tab_words"], d["tab_scales"] = pack_weight(n((K, T)) * s, "e4m3")
    d["offs"] = striped(np.random.permutation(T)[:S])
    d["offs2"] = striped(np.random.permutation(T)[:S2])
    wa = 2.5 * n((K, K)) / K / s / s.T
    d["wa_words"], d["wa_scales"] = pack_weight(wa, "e2m1")
    d["wb"] = (2.0 * n((K, K)) / K / s / s.T).astype(np.float32)
    d["prior"] = (0.6 * n(S2)).astype(np.float32)
    return d

def reference(tab_words, tab_scales, offs, offs2, wa_words, wa_scales, wb, prior):
    TW = unpack_weight(tab_words, tab_scales, "e4m3")
    v = TW[:, unstriped(offs)]
    v2 = TW[:, unstriped(offs2)]
    wa = unpack_weight(wa_words, wa_scales, "e2m1")
    wbq = mxq(f64(wb), 0, "e4m3")
    ha = np.abs(wa.T @ v)
    hb = np.maximum(wbq.T @ v, 0.0)
    haq = mxq(ha, 0, "e4m3")
    hbq = mxq(hb, 0, "e4m3")
    ea = v2.T @ haq
    eb = v2.T @ hbq
    gate = 1.0 / (1.0 + np.exp(-ea))
    return gate * eb + f64(prior)[:, None]

@@ -1,0 +1,270 @@
+from contextlib import ExitStack
+
+import concourse.mybir as mybir
+
+K, T, S, S2 = 1024, 2048, 512, 1024
+FLOPS = 2 * (2 * K * K * S + 2 * S2 * K * S)
+
+F32 = mybir.dt.float32
+BF16 = mybir.dt.bfloat16
+I32 = mybir.dt.int32
+U32 = mybir.dt.uint32
+U16 = mybir.dt.uint16
+U8 = mybir.dt.uint8
+FP8X4 = mybir.dt.float8_e4m3fn_x4
+FP4X4 = mybir.dt.float4_e2m1fn_x4
+ACT = mybir.ActivationFunctionType
+ALU = mybir.AluOpType
+
+P = 128
+PASSES = K // 512
+SLICE = 256
+
+
+def tile_list_culture_suspicion_scores_kernel(
+    tc, tab_words, tab_scales, offs, offs2, wa_words, wa_scales, wb, prior, out
+):
+    nc = tc.nc
+    with ExitStack() as ctx:
+        lists = ctx.enter_context(tc.tile_pool(name="lists", bufs=1))
+        keep = ctx.enter_context(tc.tile_pool(name="keep", bufs=1))
+        ring = ctx.enter_context(tc.tile_pool(name="ring", bufs=8))
+        stage = ctx.enter_context(tc.tile_pool(name="stage", bufs=1))
+        psum = ctx.enter_context(tc.psum_pool(name="psum", bufs=8))
+
+        def held(name, shape, dtype):
+            return keep.tile(shape, dtype, name=name, align_bytes=64)
+
+        list1 = lists.tile([P, S // 16], U16, name="list1")
+        list2 = lists.tile([P, S2 // 16], U16, name="list2")
+
+        tab_sc = held("tab_sc", [P, T // 4], I32)
+        wa_sc_raw = held("wa_sc_raw", [P, K // 4], I32)
+        v1_sc_low = held("v1_sc_low", [P, S // 4], I32)
+        wa_sc_low = held("wa_sc_low", [P, K // 4], I32)
+        nc.vector.memset(tab_sc[:], 0)
+        nc.gpsimd.memset(wa_sc_raw[:], 0)
+        nc.gpsimd.memset(v1_sc_low[:], 0)
+        nc.gpsimd.memset(wa_sc_low[:], 0)
+
+        tab = [held("tab%d" % a, [P, T], I32) for a in range(PASSES)]
+        wa_raw = [held("wa_raw%d" % a, [P, K // 2], I32) for a in range(PASSES)]
+        wb_raw = {}
+        prior_sb = held("prior_sb", [P, S2 // P], F32)
+
+        def load_wb(a, b, pieces):
+            width = 512 // pieces
+            for piece in range(pieces):
+                c0 = 512 * b + width * piece
+                rows = wb[512 * a : 512 * (a + 1), c0 : c0 + width]
+                raw = stage.tile(
+                    [P, 4, width], F32, name="wb_raw%d%d%d" % (a, b, piece), offset=4 * 4 * (512 * a + width * piece)
+                )
+                nc.sync.dma_start(raw[:], rows.rearrange("(p j) c -> p j c", j=4))
+                for h in range(2 // pieces):
+                    wb_raw[a, b, piece + h] = raw[:, :, 256 * h : 256 * (h + 1)]
+
+        def load_tab(a):
+            nc.sync.dma_start(tab[a][:], tab_words[a].rearrange("p t i -> p (t i)").bitcast(I32))
+
+        nc.sync.dma_start(list1[:], offs)
+        nc.sync.dma_start(wa_raw[0][:], wa_words[0].bitcast(I32))
+        for q in range(4):
+            nc.sync.dma_start(tab_sc[32 * q : 32 * q + 8, :], tab_scales[:, 4 * q : 4 * q + 4, :].bitcast(I32))
+        load_tab(0)
+        for q in range(4):
+            nc.sync.dma_start(wa_sc_raw[32 * q : 32 * q + 8, :], wa_scales[:, 4 * q : 4 * q + 4, :].bitcast(I32))
+        nc.sync.dma_start(list2[:], offs2)
+        load_wb(0, 0, 2)
+        nc.sync.dma_start(wa_raw[1][:], wa_words[1].bitcast(I32))
+        load_wb(1, 0, 1)
+        load_tab(1)
+
+        v1_sc = held("v1_sc", [P, S], U8)
+        v1 = [held("v1_%d" % a, [P, S], U32) for a in range(PASSES)]
+        wa_sc = held("wa_sc", [P, K], U8)
+        wa = [held("wa%d" % a, [P, 2 * K], U8) for a in range(PASSES)]
+
+        def gather_words(dst, a, lst, s):
+            nc.vector.tensor_copy(dst, tab[a][:].bitcast(U32).indirect(lst[:, 16 * s : 16 * (s + 1)]))
+
+        def gather_scales(dst, src, lst, s0, s1):
+            nc.vector.tensor_copy(dst, src[:].bitcast(U8).indirect(lst[:, 16 * s0 : 16 * s1]))
+
+        def deal_wa(a):
+            nc.vector.tensor_copy(
+                wa[a][:].bitcast(U16).rearrange("p (b t m) -> p b t m", b=2, t=4),
+                wa_raw[a][:].bitcast(U16).rearrange("p (b m t) -> p b t m", b=2, t=4),
+            )
+
+        gather_scales(v1_sc[:], tab_sc, list1, 0, 2)
+        nc.sync.dma_start(v1_sc_low[0:100, :], v1_sc[4:104, :].bitcast(I32))
+        deal_wa(0)
+        gather_words(v1[0][:, 0:SLICE], 0, list1, 0)
+        nc.vector.tensor_copy(
+            wa_sc[:].rearrange("p (b t m) -> p b t m", b=2, t=4),
+            wa_sc_raw[:].bitcast(U8).rearrange("p (b m t) -> p b t m", b=2, t=4),
+        )
+        nc.sync.dma_start(wa_sc_low[0:100, :], wa_sc[4:104, :].bitcast(I32))
+        gather_words(v1[0][:, SLICE : 2 * SLICE], 0, list1, 1)
+
+        v1_planes = [v1_sc[:], v1_sc_low[:].bitcast(U8)]
+        wa_planes = [wa_sc[:], wa_sc_low[:].bitcast(U8)]
+
+        wb_bf = {}
+        wb_q = {}
+        wb_s = {}
+        for key in [(a, b) for b in range(PASSES) for a in range(PASSES)]:
+            wb_bf[key] = held("wb_bf%d%d" % key, [P, 4, P, 4], BF16)
+            wb_q[key] = held("wb_q%d%d" % key, [P, 512], U32)
+            wb_s[key] = held("wb_s%d%d" % key, [P, 512], U8)
+
+        def cast_wb(a, b, h, on_vector):
+            src = wb_raw[a, b, h].rearrange("p j (m t) -> p m j t", t=4)
+            dst = wb_bf[a, b][:, :, 64 * h : 64 * (h + 1), :].rearrange("p t m j -> p m j t")
+            if on_vector:
+                nc.vector.tensor_copy(dst, src)
+            else:
+                nc.scalar.copy(dst, src)
+
+        def quantize_wb(a, b):
+            nc.vector.quantize_mx(
+                out=wb_q[a, b][:].bitcast(FP8X4),
+                scales=wb_s[a, b][:],
+                in_=wb_bf[a, b][:].rearrange("p t m j -> p (t m j)"),
+            )
+
+        def stage1_pass(bank, x, a, b, jc):
+            cols = slice(P * jc, P * (jc + 1))
+            for t in range(4):
+                c0 = 512 * b + P * t
+                if x == 0:
+                    w = wa[a][:, 2 * c0 : 2 * (c0 + P)].bitcast(FP4X4)
+                    ws = wa_planes[a][:, c0 : c0 + P]
+                else:
+                    w = wb_q[a, b][:, P * t : P * (t + 1)].bitcast(FP8X4)
+                    ws = wb_s[a, b][:, P * t : P * (t + 1)]
+                nc.tensor.matmul_mx(
+                    out=bank[:, P * t : P * (t + 1)],
+                    lhsT=w,
+                    lhsT_scale=ws,
+                    rhs=v1[a][:, cols].bitcast(FP8X4),
+                    rhs_scale=v1_planes[a][:, cols],
+                    start=(a == 0 and t == 0),
+                    stop=(a == PASSES - 1 and t == 3),
+                )
+
+        h_bf = {}
+        h_q = {}
+        h_s = {}
+        for x in range(2):
+            for b in range(PASSES):
+                h_bf[x, b] = held("h_bf%d%d" % (x, b), [P, S, 4], BF16)
+                h_q[x, b] = held("h_q%d%d" % (x, b), [P, S], U32)
+                h_s[x, b] = held("h_s%d%d" % (x, b), [P, S], U8)
+
+        def empty_stage1(bank, x, b, jc):
+            nc.scalar.activation(
+                h_bf[x, b][:, P * jc : P * (jc + 1), :],
+                bank[:].rearrange("p (t n) -> p n t", t=4),
+                ACT.Abs if x == 0 else ACT.Relu,
+            )
+
+        def quantize_h(x, b):
+            nc.vector.quantize_mx(
+                out=h_q[x, b][:].bitcast(FP8X4),
+                scales=h_s[x, b][:],
+                in_=h_bf[x, b][:].rearrange("p n t -> p (n t)"),
+            )
+
+        banks = {}
+
+        def first_pass(x, b):
+            for jc in range(4):
+                banks[x, b, jc] = psum.tile([P, 512], F32, name="bank")
+                stage1_pass(banks[x, b, jc], x, 0, b, jc)
+
+        def second_pass(x, b):
+            for jc in range(4):
+                stage1_pass(banks[x, b, jc], x, 1, b, jc)
+                empty_stage1(banks[x, b, jc], x, b, jc)
+
+        v2 = {}
+        v2_sc = {}
+
+        def gather_banked_scales(s):
+            v2_sc[s] = held("v2_sc%d" % s, [P, SLICE], U8)
+            gather_scales(v2_sc[s][:], tab_sc, list2, s, s + 1)
+
+        def gather_banked(a, s):
+            v2[a, s] = held("v2_%d%d" % (a, s), [P, SLICE], U32)
+            gather_words(v2[a, s][:], a, list2, s)
+
+        def stage2(x, mt):
+            bank = psum.tile([P, 512], F32, name="bank")
+            s, half = divmod(mt, 2)
+            cols = slice(P * half, P * (half + 1))
+            for b in range(PASSES):
+                nc.tensor.matmul_mx(
+                    out=bank[:],
+                    lhsT=v2[b, s][:, cols].bitcast(FP8X4),
+                    lhsT_scale=v2_sc[s][4 * b : P, cols],
+                    rhs=h_q[x, b][:].bitcast(FP8X4),
+                    rhs_scale=h_s[x, b][:],
+                    start=(b == 0),
+                    stop=(b == PASSES - 1),
+                )
+            return bank
+
+        gates = []
+
+        def gate(mt):
+            bank = stage2(0, mt)
+            g = held("gate%d" % mt, [P, S], F32)
+            nc.scalar.activation(g[:], bank[:], ACT.Sigmoid)
+            gates.append(g)
+
+        first_pass(0, 0)
+        for h in range(2):
+            cast_wb(0, 0, h, False)
+        load_wb(0, 1, 1)
+        quantize_wb(0, 0)
+        deal_wa(1)
+        first_pass(1, 0)
+        for h in range(2):
+            cast_wb(1, 0, h, False)
+        load_wb(1, 1, 2)
+        with nc.allow_non_contiguous_dma(reason="one value a partition"):
+            nc.sync.dma_start(prior_sb[:], prior.rearrange("(c p) -> p c", p=P))
+        for s in range(S // SLICE):
+            gather_words(v1[1][:, SLICE * s : SLICE * (s + 1)], 1, list1, s)
+        second_pass(0, 0)
+        quantize_wb(1, 0)
+        second_pass(1, 0)
+        first_pass(0, 1)
+        quantize_h(0, 0)
+        cast_wb(0, 1, 0, True)
+        cast_wb(0, 1, 1, True)
+        quantize_wb(0, 1)
+        second_pass(0, 1)
+        first_pass(1, 1)
+        cast_wb(1, 1, 0, True)
+        cast_wb(1, 1, 1, True)
+        quantize_wb(1, 1)
+        quantize_h(1, 0)
+        second_pass(1, 1)
+        quantize_h(0, 1)
+        quantize_h(1, 1)
+        for s in range(S2 // SLICE):
+            gather_banked_scales(s)
+            gather_banked(0, s)
+        for mt in range(8):
+            if mt % 2 == 0:
+                gather_banked(1, mt // 2)
+            gate(mt)
+            bank = stage2(1, mt)
+            prod = ring.tile([P, S], F32, name="prod")
+            nc.vector.tensor_tensor(prod[:], bank[:], gates[mt][:], ALU.mult)
+            res = ring.tile([P, S], F32, name="res")
+            nc.scalar.activation(res[:], prod[:], ACT.Identity, bias=prior_sb[:, mt : mt + 1])
+            nc.sync.dma_start(out[P * mt : P * (mt + 1), :], res[:])

@@ -19,6 +19,7 @@ ALU = mybir.AluOpType
 P = 128
 PASSES = K // 512
 SLICE = 256
+ADD_ON_VECTOR = (4, 6, 7)
 
 
 def tile_list_culture_suspicion_scores_kernel(
@@ -29,11 +30,22 @@ def tile_list_culture_suspicion_scores_kernel(
         lists = ctx.enter_context(tc.tile_pool(name="lists", bufs=1))
         keep = ctx.enter_context(tc.tile_pool(name="keep", bufs=1))
         ring = ctx.enter_context(tc.tile_pool(name="ring", bufs=8))
-        stage = ctx.enter_context(tc.tile_pool(name="stage", bufs=1))
+        reuse = ctx.enter_context(tc.tile_pool(name="reuse", bufs=1))
         psum = ctx.enter_context(tc.psum_pool(name="psum", bufs=8))
 
         def held(name, shape, dtype):
             return keep.tile(shape, dtype, name=name, align_bytes=64)
+
+        def placed(name, shape, dtype, offset):
+            if offset is None:
+                return held(name, shape, dtype)
+            return reuse.tile(shape, dtype, name=name, offset=offset, align_bytes=64)
+
+        shared = {"wb_bf10": 0, "wb_bf11": 4096, "h_bf01": 8192, "h_bf11": 12288}
+
+        warm = held("warm", [P, 2], F32)
+        nc.gpsimd.memset(warm[:, 0:1], 0.0)
+        nc.scalar.activation(warm[:, 1:2], warm[:, 0:1], ACT.Sigmoid)
 
         list1 = lists.tile([P, S // 16], U16, name="list1")
         list2 = lists.tile([P, S2 // 16], U16, name="list2")
@@ -48,21 +60,18 @@ def tile_list_culture_suspicion_scores_kernel(
         nc.gpsimd.memset(wa_sc_low[:], 0)
 
         tab = [held("tab%d" % a, [P, T], I32) for a in range(PASSES)]
-        wa_raw = [held("wa_raw%d" % a, [P, K // 2], I32) for a in range(PASSES)]
+        wa_raw = [placed("wa_raw%d" % a, [P, K // 2], I32, shared.get("wa_raw%d" % a)) for a in range(PASSES)]
         wb_raw = {}
         prior_sb = held("prior_sb", [P, S2 // P], F32)
 
-        def load_wb(a, b, pieces):
-            width = 512 // pieces
-            for piece in range(pieces):
-                c0 = 512 * b + width * piece
-                rows = wb[512 * a : 512 * (a + 1), c0 : c0 + width]
-                raw = stage.tile(
-                    [P, 4, width], F32, name="wb_raw%d%d%d" % (a, b, piece), offset=4 * 4 * (512 * a + width * piece)
-                )
-                nc.sync.dma_start(raw[:], rows.rearrange("(p j) c -> p j c", j=4))
-                for h in range(2 // pieces):
-                    wb_raw[a, b, piece + h] = raw[:, :, 256 * h : 256 * (h + 1)]
+        def load_wb(a, b, halves):
+            c0 = 512 * b + 256 * halves[0]
+            width = 256 * len(halves)
+            rows = wb[512 * a : 512 * (a + 1), c0 : c0 + width]
+            raw = held("wb_raw%d%d%d" % (a, b, halves[0]), [P, 4, width], F32)
+            nc.sync.dma_start(raw[:], rows.rearrange("(p j) c -> p j c", j=4))
+            for i, h in enumerate(halves):
+                wb_raw[a, b, h] = raw[:, :, 256 * i : 256 * (i + 1)]
 
         def load_tab(a):
             nc.sync.dma_start(tab[a][:], tab_words[a].rearrange("p t i -> p (t i)").bitcast(I32))
@@ -71,17 +80,15 @@ def tile_list_culture_suspicion_scores_kernel(
         nc.sync.dma_start(wa_raw[0][:], wa_words[0].bitcast(I32))
         for q in range(4):
             nc.sync.dma_start(tab_sc[32 * q : 32 * q + 8, :], tab_scales[:, 4 * q : 4 * q + 4, :].bitcast(I32))
+        nc.sync.dma_start(list2[:], offs2)
+        load_wb(0, 0, [0, 1])
         load_tab(0)
         for q in range(4):
             nc.sync.dma_start(wa_sc_raw[32 * q : 32 * q + 8, :], wa_scales[:, 4 * q : 4 * q + 4, :].bitcast(I32))
-        nc.sync.dma_start(list2[:], offs2)
-        load_wb(0, 0, 2)
-        nc.sync.dma_start(wa_raw[1][:], wa_words[1].bitcast(I32))
-        load_wb(1, 0, 1)
-        load_tab(1)
+        load_wb(1, 0, [0])
 
         v1_sc = held("v1_sc", [P, S], U8)
-        v1 = [held("v1_%d" % a, [P, S], U32) for a in range(PASSES)]
+        v1 = [held("v1_0", [P, S], U32), placed("v1_1", [P, S], U32, shared["wb_bf10"])]
         wa_sc = held("wa_sc", [P, K], U8)
         wa = [held("wa%d" % a, [P, 2 * K], U8) for a in range(PASSES)]
 
@@ -97,16 +104,15 @@ def tile_list_culture_suspicion_scores_kernel(
                 wa_raw[a][:].bitcast(U16).rearrange("p (b m t) -> p b t m", b=2, t=4),
             )
 
-        gather_scales(v1_sc[:], tab_sc, list1, 0, 2)
-        nc.sync.dma_start(v1_sc_low[0:100, :], v1_sc[4:104, :].bitcast(I32))
-        deal_wa(0)
-        gather_words(v1[0][:, 0:SLICE], 0, list1, 0)
-        nc.vector.tensor_copy(
-            wa_sc[:].rearrange("p (b t m) -> p b t m", b=2, t=4),
-            wa_sc_raw[:].bitcast(U8).rearrange("p (b m t) -> p b t m", b=2, t=4),
-        )
-        nc.sync.dma_start(wa_sc_low[0:100, :], wa_sc[4:104, :].bitcast(I32))
-        gather_words(v1[0][:, SLICE : 2 * SLICE], 0, list1, 1)
+        def deal_wa_scales(b):
+            cols = slice(512 * b, 512 * (b + 1))
+            nc.vector.tensor_copy(
+                wa_sc[:, cols].rearrange("p (t m) -> p t m", t=4),
+                wa_sc_raw[:].bitcast(U8)[:, cols].rearrange("p (m t) -> p t m", t=4),
+            )
+
+        def gather_incoming(a, s):
+            gather_words(v1[a][:, SLICE * s : SLICE * (s + 1)], a, list1, s)
 
         v1_planes = [v1_sc[:], v1_sc_low[:].bitcast(U8)]
         wa_planes = [wa_sc[:], wa_sc_low[:].bitcast(U8)]
@@ -115,7 +121,7 @@ def tile_list_culture_suspicion_scores_kernel(
         wb_q = {}
         wb_s = {}
         for key in [(a, b) for b in range(PASSES) for a in range(PASSES)]:
-            wb_bf[key] = held("wb_bf%d%d" % key, [P, 4, P, 4], BF16)
+            wb_bf[key] = placed("wb_bf%d%d" % key, [P, 4, P, 4], BF16, shared.get("wb_bf%d%d" % key))
             wb_q[key] = held("wb_q%d%d" % key, [P, 512], U32)
             wb_s[key] = held("wb_s%d%d" % key, [P, 512], U8)
 
@@ -149,7 +155,7 @@ def tile_list_culture_suspicion_scores_kernel(
                     lhsT=w,
                     lhsT_scale=ws,
                     rhs=v1[a][:, cols].bitcast(FP8X4),
-                    rhs_scale=v1_planes[a][:, cols],
+                    rhs_scale=v1_planes[a][:, cols] if x == 0 else v1_sc[4 * a : P, cols],
                     start=(a == 0 and t == 0),
                     stop=(a == PASSES - 1 and t == 3),
                 )
@@ -159,7 +165,7 @@ def tile_list_culture_suspicion_scores_kernel(
         h_s = {}
         for x in range(2):
             for b in range(PASSES):
-                h_bf[x, b] = held("h_bf%d%d" % (x, b), [P, S, 4], BF16)
+                h_bf[x, b] = placed("h_bf%d%d" % (x, b), [P, S, 4], BF16, shared.get("h_bf%d%d" % (x, b)))
                 h_q[x, b] = held("h_q%d%d" % (x, b), [P, S], U32)
                 h_s[x, b] = held("h_s%d%d" % (x, b), [P, S], U8)
 
@@ -192,12 +198,12 @@ def tile_list_culture_suspicion_scores_kernel(
         v2 = {}
         v2_sc = {}
 
-        def gather_banked_scales(s):
-            v2_sc[s] = held("v2_sc%d" % s, [P, SLICE], U8)
+        def gather_banked_scales(s, offset=None):
+            v2_sc[s] = placed("v2_sc%d" % s, [P, SLICE], U8, offset)
             gather_scales(v2_sc[s][:], tab_sc, list2, s, s + 1)
 
-        def gather_banked(a, s):
-            v2[a, s] = held("v2_%d%d" % (a, s), [P, SLICE], U32)
+        def gather_banked(a, s, offset=None):
+            v2[a, s] = placed("v2_%d%d" % (a, s), [P, SLICE], U32, offset)
             gather_words(v2[a, s][:], a, list2, s)
 
         def stage2(x, mt):
@@ -224,47 +230,91 @@ def tile_list_culture_suspicion_scores_kernel(
             nc.scalar.activation(g[:], bank[:], ACT.Sigmoid)
             gates.append(g)
 
-        first_pass(0, 0)
-        for h in range(2):
-            cast_wb(0, 0, h, False)
-        load_wb(0, 1, 1)
+        gather_scales(v1_sc[:], tab_sc, list1, 0, 2)
+        nc.sync.dma_start(v1_sc_low[0:100, :], v1_sc[4:104, :].bitcast(I32))
+        load_wb(1, 0, [1])
+        load_tab(1)
+        nc.sync.dma_start(wa_raw[1][:], wa_words[1].bitcast(I32))
+        cast_wb(0, 0, 0, False)
+        cast_wb(0, 0, 1, False)
+        deal_wa(0)
+        for s in range(4):
+            gather_banked_scales(s)
+        gather_incoming(0, 0)
         quantize_wb(0, 0)
-        deal_wa(1)
+        gather_incoming(0, 1)
         first_pass(1, 0)
-        for h in range(2):
-            cast_wb(1, 0, h, False)
-        load_wb(1, 1, 2)
+        deal_wa_scales(0)
+        deal_wa_scales(1)
+        nc.sync.dma_start(wa_sc_low[0:100, :], wa_sc[4:104, :].bitcast(I32))
+        load_wb(0, 1, [0, 1])
+        load_wb(1, 1, [0, 1])
         with nc.allow_non_contiguous_dma(reason="one value a partition"):
             nc.sync.dma_start(prior_sb[:], prior.rearrange("(c p) -> p c", p=P))
-        for s in range(S // SLICE):
-            gather_words(v1[1][:, SLICE * s : SLICE * (s + 1)], 1, list1, s)
-        second_pass(0, 0)
+        first_pass(0, 0)
+        cast_wb(1, 0, 0, False)
+        cast_wb(1, 0, 1, False)
+        gather_banked(0, 0)
+        gather_banked(0, 1)
         quantize_wb(1, 0)
+        gather_incoming(1, 0)
+        gather_incoming(1, 1)
+        deal_wa(1)
         second_pass(1, 0)
-        first_pass(0, 1)
-        quantize_h(0, 0)
+        second_pass(0, 0)
         cast_wb(0, 1, 0, True)
         cast_wb(0, 1, 1, True)
         quantize_wb(0, 1)
+        first_pass(0, 1)
         second_pass(0, 1)
-        first_pass(1, 1)
+        quantize_h(1, 0)
         cast_wb(1, 1, 0, True)
         cast_wb(1, 1, 1, True)
         quantize_wb(1, 1)
-        quantize_h(1, 0)
+        first_pass(1, 1)
         second_pass(1, 1)
+        quantize_h(0, 0)
+        gather_banked(1, 0, shared["wb_bf11"])
         quantize_h(0, 1)
+        gate(0)
+        gate(1)
+        gather_banked(1, 1, shared["h_bf01"])
+        gate(2)
+        gate(3)
+        gather_banked(0, 2, shared["h_bf01"] + 1024)
         quantize_h(1, 1)
-        for s in range(S2 // SLICE):
-            gather_banked_scales(s)
-            gather_banked(0, s)
-        for mt in range(8):
-            if mt % 2 == 0:
-                gather_banked(1, mt // 2)
-            gate(mt)
-            bank = stage2(1, mt)
+        gather_banked(1, 2, shared["h_bf11"])
+
+        matches = {}
+
+        def finish(mt):
             prod = ring.tile([P, S], F32, name="prod")
-            nc.vector.tensor_tensor(prod[:], bank[:], gates[mt][:], ALU.mult)
+            nc.vector.tensor_tensor(prod[:], matches[mt][:], gates[mt][:], ALU.mult)
             res = ring.tile([P, S], F32, name="res")
-            nc.scalar.activation(res[:], prod[:], ACT.Identity, bias=prior_sb[:, mt : mt + 1])
+            if mt in ADD_ON_VECTOR:
+                nc.vector.tensor_scalar(res[:], prod[:], prior_sb[:, mt : mt + 1], None, ALU.add)
+            else:
+                nc.scalar.activation(res[:], prod[:], ACT.Identity, bias=prior_sb[:, mt : mt + 1])
             nc.sync.dma_start(out[P * mt : P * (mt + 1), :], res[:])
+
+        for mt in range(2):
+            matches[mt] = stage2(1, mt)
+        finish(0)
+        gate(4)
+        gate(5)
+        finish(1)
+        for mt in range(2, 4):
+            matches[mt] = stage2(1, mt)
+        for a in range(PASSES):
+            gather_banked(a, 3, shared["h_bf11"] + 1024 * (a + 1))
+        finish(2)
+        finish(3)
+        for mt in range(4, 6):
+            matches[mt] = stage2(1, mt)
+        gate(6)
+        gate(7)
+        finish(4)
+        finish(5)
+        for mt in range(6, 8):
+            matches[mt] = stage2(1, mt)
+            finish(mt)

@@ -19,7 +19,6 @@ ALU = mybir.AluOpType
 P = 128
 PASSES = K // 512
 SLICE = 256
-ADD_ON_VECTOR = (4, 6, 7)
 
 
 def tile_list_culture_suspicion_scores_kernel(
@@ -70,6 +69,7 @@ def tile_list_culture_suspicion_scores_kernel(
             rows = wb[512 * a : 512 * (a + 1), c0 : c0 + width]
             raw = held("wb_raw%d%d%d" % (a, b, halves[0]), [P, 4, width], F32)
             nc.sync.dma_start(raw[:], rows.rearrange("(p j) c -> p j c", j=4))
+            wb_raw[a, b] = raw[:]
             for i, h in enumerate(halves):
                 wb_raw[a, b, h] = raw[:, :, 256 * i : 256 * (i + 1)]
 
@@ -104,11 +104,10 @@ def tile_list_culture_suspicion_scores_kernel(
                 wa_raw[a][:].bitcast(U16).rearrange("p (b m t) -> p b t m", b=2, t=4),
             )
 
-        def deal_wa_scales(b):
-            cols = slice(512 * b, 512 * (b + 1))
+        def deal_wa_scales():
             nc.vector.tensor_copy(
-                wa_sc[:, cols].rearrange("p (t m) -> p t m", t=4),
-                wa_sc_raw[:].bitcast(U8)[:, cols].rearrange("p (m t) -> p t m", t=4),
+                wa_sc[:].rearrange("p (b t m) -> p b t m", b=2, t=4),
+                wa_sc_raw[:].bitcast(U8).rearrange("p (b m t) -> p b t m", b=2, t=4),
             )
 
         def gather_incoming(a, s):
@@ -125,13 +124,14 @@ def tile_list_culture_suspicion_scores_kernel(
             wb_q[key] = held("wb_q%d%d" % key, [P, 512], U32)
             wb_s[key] = held("wb_s%d%d" % key, [P, 512], U8)
 
-        def cast_wb(a, b, h, on_vector):
+        def cast_half_on_scalar(a, b, h):
             src = wb_raw[a, b, h].rearrange("p j (m t) -> p m j t", t=4)
             dst = wb_bf[a, b][:, :, 64 * h : 64 * (h + 1), :].rearrange("p t m j -> p m j t")
-            if on_vector:
-                nc.vector.tensor_copy(dst, src)
-            else:
-                nc.scalar.copy(dst, src)
+            nc.scalar.copy(dst, src)
+
+        def cast_block_on_vector(a, b):
+            src = wb_raw[a, b].rearrange("p j (m t) -> p m j t", t=4)
+            nc.vector.tensor_copy(wb_bf[a, b][:].rearrange("p t m j -> p m j t"), src)
 
         def quantize_wb(a, b):
             nc.vector.quantize_mx(
@@ -176,18 +176,24 @@ def tile_list_culture_suspicion_scores_kernel(
                 ACT.Abs if x == 0 else ACT.Relu,
             )
 
-        def quantize_h(x, b):
-            nc.vector.quantize_mx(
-                out=h_q[x, b][:].bitcast(FP8X4),
-                scales=h_s[x, b][:],
-                in_=h_bf[x, b][:].rearrange("p n t -> p (n t)"),
-            )
+        def quantize_h(x, b, pieces=1):
+            width = S // pieces
+            for piece in range(pieces):
+                cols = slice(width * piece, width * (piece + 1))
+                nc.vector.quantize_mx(
+                    out=h_q[x, b][:, cols].bitcast(FP8X4),
+                    scales=h_s[x, b][:, cols],
+                    in_=h_bf[x, b][:, cols, :].rearrange("p n t -> p (n t)"),
+                )
 
         banks = {}
 
-        def first_pass(x, b):
+        def take_banks(x, b):
             for jc in range(4):
                 banks[x, b, jc] = psum.tile([P, 512], F32, name="bank")
+
+        def first_pass(x, b):
+            for jc in range(4):
                 stage1_pass(banks[x, b, jc], x, 0, b, jc)
 
         def second_pass(x, b):
@@ -196,11 +202,7 @@ def tile_list_culture_suspicion_scores_kernel(
                 empty_stage1(banks[x, b, jc], x, b, jc)
 
         v2 = {}
-        v2_sc = {}
-
-        def gather_banked_scales(s, offset=None):
-            v2_sc[s] = placed("v2_sc%d" % s, [P, SLICE], U8, offset)
-            gather_scales(v2_sc[s][:], tab_sc, list2, s, s + 1)
+        v2_sc = held("v2_sc", [P, S2], U8)
 
         def gather_banked(a, s, offset=None):
             v2[a, s] = placed("v2_%d%d" % (a, s), [P, SLICE], U32, offset)
@@ -214,7 +216,7 @@ def tile_list_culture_suspicion_scores_kernel(
                 nc.tensor.matmul_mx(
                     out=bank[:],
                     lhsT=v2[b, s][:, cols].bitcast(FP8X4),
-                    lhsT_scale=v2_sc[s][4 * b : P, cols],
+                    lhsT_scale=v2_sc[4 * b : P, P * mt : P * (mt + 1)],
                     rhs=h_q[x, b][:].bitcast(FP8X4),
                     rhs_scale=h_s[x, b][:],
                     start=(b == 0),
@@ -235,86 +237,83 @@ def tile_list_culture_suspicion_scores_kernel(
         load_wb(1, 0, [1])
         load_tab(1)
         nc.sync.dma_start(wa_raw[1][:], wa_words[1].bitcast(I32))
-        cast_wb(0, 0, 0, False)
-        cast_wb(0, 0, 1, False)
+        cast_half_on_scalar(0, 0, 0)
+        cast_half_on_scalar(0, 0, 1)
         deal_wa(0)
-        for s in range(4):
-            gather_banked_scales(s)
+        gather_scales(v2_sc[:], tab_sc, list2, 0, 4)
         gather_incoming(0, 0)
         quantize_wb(0, 0)
         gather_incoming(0, 1)
+        take_banks(1, 0)
         first_pass(1, 0)
-        deal_wa_scales(0)
-        deal_wa_scales(1)
+        deal_wa_scales()
         nc.sync.dma_start(wa_sc_low[0:100, :], wa_sc[4:104, :].bitcast(I32))
         load_wb(0, 1, [0, 1])
         load_wb(1, 1, [0, 1])
         with nc.allow_non_contiguous_dma(reason="one value a partition"):
             nc.sync.dma_start(prior_sb[:], prior.rearrange("(c p) -> p c", p=P))
+        take_banks(0, 0)
         first_pass(0, 0)
-        cast_wb(1, 0, 0, False)
-        cast_wb(1, 0, 1, False)
+        cast_half_on_scalar(1, 0, 0)
+        cast_half_on_scalar(1, 0, 1)
         gather_banked(0, 0)
         gather_banked(0, 1)
         quantize_wb(1, 0)
         gather_incoming(1, 0)
         gather_incoming(1, 1)
         deal_wa(1)
+        gather_banked(1, 0, shared["wb_bf10"] + 2048)
         second_pass(1, 0)
         second_pass(0, 0)
-        cast_wb(0, 1, 0, True)
-        cast_wb(0, 1, 1, True)
+        cast_block_on_vector(0, 1)
         quantize_wb(0, 1)
+        take_banks(0, 1)
         first_pass(0, 1)
         second_pass(0, 1)
         quantize_h(1, 0)
-        cast_wb(1, 1, 0, True)
-        cast_wb(1, 1, 1, True)
+        cast_block_on_vector(1, 1)
         quantize_wb(1, 1)
+        take_banks(1, 1)
         first_pass(1, 1)
         second_pass(1, 1)
         quantize_h(0, 0)
-        gather_banked(1, 0, shared["wb_bf11"])
-        quantize_h(0, 1)
-        gate(0)
-        gate(1)
-        gather_banked(1, 1, shared["h_bf01"])
-        gate(2)
-        gate(3)
-        gather_banked(0, 2, shared["h_bf01"] + 1024)
-        quantize_h(1, 1)
-        gather_banked(1, 2, shared["h_bf11"])
+        gather_banked(1, 1, shared["wb_bf11"])
+        quantize_h(0, 1, 2)
+        for mt in range(4):
+            gate(mt)
+        for a in range(PASSES):
+            gather_banked(a, 2, shared["h_bf01"] + 1024 * a)
+        quantize_h(1, 1, 2)
 
         matches = {}
 
-        def finish(mt):
-            prod = ring.tile([P, S], F32, name="prod")
-            nc.vector.tensor_tensor(prod[:], matches[mt][:], gates[mt][:], ALU.mult)
-            res = ring.tile([P, S], F32, name="res")
-            if mt in ADD_ON_VECTOR:
-                nc.vector.tensor_scalar(res[:], prod[:], prior_sb[:, mt : mt + 1], None, ALU.add)
-            else:
-                nc.scalar.activation(res[:], prod[:], ACT.Identity, bias=prior_sb[:, mt : mt + 1])
-            nc.sync.dma_start(out[P * mt : P * (mt + 1), :], res[:])
+        def finish(mt, pieces=1):
+            width = S // pieces
+            for piece in range(pieces):
+                cols = slice(width * piece, width * (piece + 1))
+                prod = ring.tile([P, width], F32, name="prod")
+                nc.vector.tensor_tensor(prod[:], matches[mt][:, cols], gates[mt][:, cols], ALU.mult)
+                res = ring.tile([P, width], F32, name="res")
+                if mt == 7:
+                    nc.vector.tensor_scalar(res[:], prod[:], prior_sb[:, mt : mt + 1], None, ALU.add)
+                else:
+                    nc.scalar.activation(res[:], prod[:], ACT.Identity, bias=prior_sb[:, mt : mt + 1])
+                nc.sync.dma_start(out[P * mt : P * (mt + 1), cols], res[:])
 
+        for a in range(PASSES):
+            gather_banked(a, 3, shared["h_bf11"] + 1024 * a)
         for mt in range(2):
             matches[mt] = stage2(1, mt)
-        finish(0)
         gate(4)
         gate(5)
+        finish(0)
         finish(1)
         for mt in range(2, 4):
             matches[mt] = stage2(1, mt)
-        for a in range(PASSES):
-            gather_banked(a, 3, shared["h_bf11"] + 1024 * (a + 1))
-        finish(2)
-        finish(3)
-        for mt in range(4, 6):
-            matches[mt] = stage2(1, mt)
         gate(6)
         gate(7)
-        finish(4)
-        finish(5)
-        for mt in range(6, 8):
+        finish(2)
+        finish(3)
+        for mt in range(4, 8):
             matches[mt] = stage2(1, mt)
-            finish(mt)
+            finish(mt, 2 if mt == 7 else 1)

from contextlib import ExitStack

import concourse.mybir as mybir

K, T, S, S2 = 1024, 2048, 512, 1024
FLOPS = 2 * (2 * K * K * S + 2 * S2 * K * S)

F32 = mybir.dt.float32
BF16 = mybir.dt.bfloat16
I32 = mybir.dt.int32
U32 = mybir.dt.uint32
U16 = mybir.dt.uint16
U8 = mybir.dt.uint8
FP8X4 = mybir.dt.float8_e4m3fn_x4
FP4X4 = mybir.dt.float4_e2m1fn_x4
ACT = mybir.ActivationFunctionType
ALU = mybir.AluOpType

P = 128
PASSES = K // 512
SLICE = 256


def tile_list_culture_suspicion_scores_kernel(
    tc, tab_words, tab_scales, offs, offs2, wa_words, wa_scales, wb, prior, out
):
    nc = tc.nc
    with ExitStack() as ctx:
        lists = ctx.enter_context(tc.tile_pool(name="lists", bufs=1))
        keep = ctx.enter_context(tc.tile_pool(name="keep", bufs=1))
        ring = ctx.enter_context(tc.tile_pool(name="ring", bufs=8))
        reuse = ctx.enter_context(tc.tile_pool(name="reuse", bufs=1))
        psum = ctx.enter_context(tc.psum_pool(name="psum", bufs=8))

        def held(name, shape, dtype):
            return keep.tile(shape, dtype, name=name, align_bytes=64)

        def placed(name, shape, dtype, offset):
            if offset is None:
                return held(name, shape, dtype)
            return reuse.tile(shape, dtype, name=name, offset=offset, align_bytes=64)

        shared = {"wb_bf10": 0, "wb_bf11": 4096, "h_bf01": 8192, "h_bf11": 12288}

        warm = held("warm", [P, 2], F32)
        nc.gpsimd.memset(warm[:, 0:1], 0.0)
        nc.scalar.activation(warm[:, 1:2], warm[:, 0:1], ACT.Sigmoid)

        list1 = lists.tile([P, S // 16], U16, name="list1")
        list2 = lists.tile([P, S2 // 16], U16, name="list2")

        tab_sc = held("tab_sc", [P, T // 4], I32)
        wa_sc_raw = held("wa_sc_raw", [P, K // 4], I32)
        v1_sc_low = held("v1_sc_low", [P, S // 4], I32)
        wa_sc_low = held("wa_sc_low", [P, K // 4], I32)
        nc.vector.memset(tab_sc[:], 0)
        nc.gpsimd.memset(wa_sc_raw[:], 0)
        nc.gpsimd.memset(v1_sc_low[:], 0)
        nc.gpsimd.memset(wa_sc_low[:], 0)

        tab = [held("tab%d" % a, [P, T], I32) for a in range(PASSES)]
        wa_raw = [placed("wa_raw%d" % a, [P, K // 2], I32, shared.get("wa_raw%d" % a)) for a in range(PASSES)]
        wb_raw = {}
        prior_sb = held("prior_sb", [P, S2 // P], F32)

        def load_wb(a, b, halves):
            c0 = 512 * b + 256 * halves[0]
            width = 256 * len(halves)
            rows = wb[512 * a : 512 * (a + 1), c0 : c0 + width]
            raw = held("wb_raw%d%d%d" % (a, b, halves[0]), [P, 4, width], F32)
            nc.sync.dma_start(raw[:], rows.rearrange("(p j) c -> p j c", j=4))
            wb_raw[a, b] = raw[:]
            for i, h in enumerate(halves):
                wb_raw[a, b, h] = raw[:, :, 256 * i : 256 * (i + 1)]

        def load_tab(a):
            nc.sync.dma_start(tab[a][:], tab_words[a].rearrange("p t i -> p (t i)").bitcast(I32))

        nc.sync.dma_start(list1[:], offs)
        nc.sync.dma_start(wa_raw[0][:], wa_words[0].bitcast(I32))
        for q in range(4):
            nc.sync.dma_start(tab_sc[32 * q : 32 * q + 8, :], tab_scales[:, 4 * q : 4 * q + 4, :].bitcast(I32))
        nc.sync.dma_start(list2[:], offs2)
        load_wb(0, 0, [0, 1])
        load_tab(0)
        for q in range(4):
            nc.sync.dma_start(wa_sc_raw[32 * q : 32 * q + 8, :], wa_scales[:, 4 * q : 4 * q + 4, :].bitcast(I32))
        load_wb(1, 0, [0])

        v1_sc = held("v1_sc", [P, S], U8)
        v1 = [held("v1_0", [P, S], U32), placed("v1_1", [P, S], U32, shared["wb_bf10"])]
        wa_sc = held("wa_sc", [P, K], U8)
        wa = [held("wa%d" % a, [P, 2 * K], U8) for a in range(PASSES)]

        def gather_words(dst, a, lst, s):
            nc.vector.tensor_copy(dst, tab[a][:].bitcast(U32).indirect(lst[:, 16 * s : 16 * (s + 1)]))

        def gather_scales(dst, src, lst, s0, s1):
            nc.vector.tensor_copy(dst, src[:].bitcast(U8).indirect(lst[:, 16 * s0 : 16 * s1]))

        def deal_wa(a):
            nc.vector.tensor_copy(
                wa[a][:].bitcast(U16).rearrange("p (b t m) -> p b t m", b=2, t=4),
                wa_raw[a][:].bitcast(U16).rearrange("p (b m t) -> p b t m", b=2, t=4),
            )

        def deal_wa_scales():
            nc.vector.tensor_copy(
                wa_sc[:].rearrange("p (b t m) -> p b t m", b=2, t=4),
                wa_sc_raw[:].bitcast(U8).rearrange("p (b m t) -> p b t m", b=2, t=4),
            )

        def gather_incoming(a, s):
            gather_words(v1[a][:, SLICE * s : SLICE * (s + 1)], a, list1, s)

        v1_planes = [v1_sc[:], v1_sc_low[:].bitcast(U8)]
        wa_planes = [wa_sc[:], wa_sc_low[:].bitcast(U8)]

        wb_bf = {}
        wb_q = {}
        wb_s = {}
        for key in [(a, b) for b in range(PASSES) for a in range(PASSES)]:
            wb_bf[key] = placed("wb_bf%d%d" % key, [P, 4, P, 4], BF16, shared.get("wb_bf%d%d" % key))
            wb_q[key] = held("wb_q%d%d" % key, [P, 512], U32)
            wb_s[key] = held("wb_s%d%d" % key, [P, 512], U8)

        def cast_half_on_scalar(a, b, h):
            src = wb_raw[a, b, h].rearrange("p j (m t) -> p m j t", t=4)
            dst = wb_bf[a, b][:, :, 64 * h : 64 * (h + 1), :].rearrange("p t m j -> p m j t")
            nc.scalar.copy(dst, src)

        def cast_block_on_vector(a, b):
            src = wb_raw[a, b].rearrange("p j (m t) -> p m j t", t=4)
            nc.vector.tensor_copy(wb_bf[a, b][:].rearrange("p t m j -> p m j t"), src)

        def quantize_wb(a, b):
            nc.vector.quantize_mx(
                out=wb_q[a, b][:].bitcast(FP8X4),
                scales=wb_s[a, b][:],
                in_=wb_bf[a, b][:].rearrange("p t m j -> p (t m j)"),
            )

        def stage1_pass(bank, x, a, b, jc):
            cols = slice(P * jc, P * (jc + 1))
            for t in range(4):
                c0 = 512 * b + P * t
                if x == 0:
                    w = wa[a][:, 2 * c0 : 2 * (c0 + P)].bitcast(FP4X4)
                    ws = wa_planes[a][:, c0 : c0 + P]
                else:
                    w = wb_q[a, b][:, P * t : P * (t + 1)].bitcast(FP8X4)
                    ws = wb_s[a, b][:, P * t : P * (t + 1)]
                nc.tensor.matmul_mx(
                    out=bank[:, P * t : P * (t + 1)],
                    lhsT=w,
                    lhsT_scale=ws,
                    rhs=v1[a][:, cols].bitcast(FP8X4),
                    rhs_scale=v1_planes[a][:, cols] if x == 0 else v1_sc[4 * a : P, cols],
                    start=(a == 0 and t == 0),
                    stop=(a == PASSES - 1 and t == 3),
                )

        h_bf = {}
        h_q = {}
        h_s = {}
        for x in range(2):
            for b in range(PASSES):
                h_bf[x, b] = placed("h_bf%d%d" % (x, b), [P, S, 4], BF16, shared.get("h_bf%d%d" % (x, b)))
                h_q[x, b] = held("h_q%d%d" % (x, b), [P, S], U32)
                h_s[x, b] = held("h_s%d%d" % (x, b), [P, S], U8)

        def empty_stage1(bank, x, b, jc):
            nc.scalar.activation(
                h_bf[x, b][:, P * jc : P * (jc + 1), :],
                bank[:].rearrange("p (t n) -> p n t", t=4),
                ACT.Abs if x == 0 else ACT.Relu,
            )

        def quantize_h(x, b, pieces=1):
            width = S // pieces
            for piece in range(pieces):
                cols = slice(width * piece, width * (piece + 1))
                nc.vector.quantize_mx(
                    out=h_q[x, b][:, cols].bitcast(FP8X4),
                    scales=h_s[x, b][:, cols],
                    in_=h_bf[x, b][:, cols, :].rearrange("p n t -> p (n t)"),
                )

        banks = {}

        def take_banks(x, b):
            for jc in range(4):
                banks[x, b, jc] = psum.tile([P, 512], F32, name="bank")

        def first_pass(x, b):
            for jc in range(4):
                stage1_pass(banks[x, b, jc], x, 0, b, jc)

        def second_pass(x, b):
            for jc in range(4):
                stage1_pass(banks[x, b, jc], x, 1, b, jc)
                empty_stage1(banks[x, b, jc], x, b, jc)

        v2 = {}
        v2_sc = held("v2_sc", [P, S2], U8)

        def gather_banked(a, s, offset=None):
            v2[a, s] = placed("v2_%d%d" % (a, s), [P, SLICE], U32, offset)
            gather_words(v2[a, s][:], a, list2, s)

        def stage2(x, mt):
            bank = psum.tile([P, 512], F32, name="bank")
            s, half = divmod(mt, 2)
            cols = slice(P * half, P * (half + 1))
            for b in range(PASSES):
                nc.tensor.matmul_mx(
                    out=bank[:],
                    lhsT=v2[b, s][:, cols].bitcast(FP8X4),
                    lhsT_scale=v2_sc[4 * b : P, P * mt : P * (mt + 1)],
                    rhs=h_q[x, b][:].bitcast(FP8X4),
                    rhs_scale=h_s[x, b][:],
                    start=(b == 0),
                    stop=(b == PASSES - 1),
                )
            return bank

        gates = []

        def gate(mt):
            bank = stage2(0, mt)
            g = held("gate%d" % mt, [P, S], F32)
            nc.scalar.activation(g[:], bank[:], ACT.Sigmoid)
            gates.append(g)

        gather_scales(v1_sc[:], tab_sc, list1, 0, 2)
        nc.sync.dma_start(v1_sc_low[0:100, :], v1_sc[4:104, :].bitcast(I32))
        load_wb(1, 0, [1])
        load_tab(1)
        nc.sync.dma_start(wa_raw[1][:], wa_words[1].bitcast(I32))
        cast_half_on_scalar(0, 0, 0)
        cast_half_on_scalar(0, 0, 1)
        deal_wa(0)
        gather_scales(v2_sc[:], tab_sc, list2, 0, 4)
        gather_incoming(0, 0)
        quantize_wb(0, 0)
        gather_incoming(0, 1)
        take_banks(1, 0)
        first_pass(1, 0)
        deal_wa_scales()
        nc.sync.dma_start(wa_sc_low[0:100, :], wa_sc[4:104, :].bitcast(I32))
        load_wb(0, 1, [0, 1])
        load_wb(1, 1, [0, 1])
        with nc.allow_non_contiguous_dma(reason="one value a partition"):
            nc.sync.dma_start(prior_sb[:], prior.rearrange("(c p) -> p c", p=P))
        take_banks(0, 0)
        first_pass(0, 0)
        cast_half_on_scalar(1, 0, 0)
        cast_half_on_scalar(1, 0, 1)
        gather_banked(0, 0)
        gather_banked(0, 1)
        quantize_wb(1, 0)
        gather_incoming(1, 0)
        gather_incoming(1, 1)
        deal_wa(1)
        gather_banked(1, 0, shared["wb_bf10"] + 2048)
        second_pass(1, 0)
        second_pass(0, 0)
        cast_block_on_vector(0, 1)
        quantize_wb(0, 1)
        take_banks(0, 1)
        first_pass(0, 1)
        second_pass(0, 1)
        quantize_h(1, 0)
        cast_block_on_vector(1, 1)
        quantize_wb(1, 1)
        take_banks(1, 1)
        first_pass(1, 1)
        second_pass(1, 1)
        quantize_h(0, 0)
        gather_banked(1, 1, shared["wb_bf11"])
        quantize_h(0, 1, 2)
        for mt in range(4):
            gate(mt)
        for a in range(PASSES):
            gather_banked(a, 2, shared["h_bf01"] + 1024 * a)
        quantize_h(1, 1, 2)

        matches = {}

        def finish(mt, pieces=1):
            width = S // pieces
            for piece in range(pieces):
                cols = slice(width * piece, width * (piece + 1))
                prod = ring.tile([P, width], F32, name="prod")
                nc.vector.tensor_tensor(prod[:], matches[mt][:, cols], gates[mt][:, cols], ALU.mult)
                res = ring.tile([P, width], F32, name="res")
                if mt == 7:
                    nc.vector.tensor_scalar(res[:], prod[:], prior_sb[:, mt : mt + 1], None, ALU.add)
                else:
                    nc.scalar.activation(res[:], prod[:], ACT.Identity, bias=prior_sb[:, mt : mt + 1])
                nc.sync.dma_start(out[P * mt : P * (mt + 1), cols], res[:])

        for a in range(PASSES):
            gather_banked(a, 3, shared["h_bf11"] + 1024 * a)
        for mt in range(2):
            matches[mt] = stage2(1, mt)
        gate(4)
        gate(5)
        finish(0)
        finish(1)
        for mt in range(2, 4):
            matches[mt] = stage2(1, mt)
        gate(6)
        gate(7)
        finish(2)
        finish(3)
        for mt in range(4, 8):
            matches[mt] = stage2(1, mt)
            finish(mt, 2 if mt == 7 else 1)
